import numpy as np
import ml_dtypes


def mxq(x, axis, fmt="e4m3"):
    dtype, down = {"e4m3": (ml_dtypes.float8_e4m3fn, 7), "e5m2": (ml_dtypes.float8_e5m2, 14)}[fmt]
    v = np.moveaxis(np.asarray(x, np.float32).astype(ml_dtypes.bfloat16).astype(np.float64), axis, -1)
    blocks = v.reshape(v.shape[:-1] + (-1, 32))
    amax = np.abs(blocks).max(-1, keepdims=True)
    byte = np.maximum(np.where(amax > 0, np.frexp(amax)[1] - 1 + 127, 0) - down, 1)
    scale = np.exp2(byte - 127.0)
    codes = (blocks / scale).astype(np.float32).astype(dtype).astype(np.float64)
    return np.moveaxis((codes * scale).reshape(v.shape), -1, axis)


WIDE = False


def mx_kscale(k):
    if not WIDE:
        return np.ones(k)
    levels = np.array([10, -10, 5, -5, 0])
    if k % 512:
        return np.exp2(np.random.permutation(np.resize(levels, k // 32))).repeat(32)
    a = np.empty((k // 512, 16))
    for p in range(k // 512):
        a[p, :8] = np.random.permutation(np.resize(levels, 8))
        for g in range(8):
            far = levels[np.abs(levels - a[p, g]) >= 10]
            a[p, g + 8] = far[np.random.randint(len(far))]
    return np.exp2(a.ravel()).repeat(32)


def f64(x):
    return np.asarray(x).astype(np.float64)


def striped(idx):
    return np.tile(idx.reshape(-1, 16).T, (8, 1)).astype(np.uint16)


def unstriped(offs):
    return offs[:16].T.reshape(-1).astype(np.int64)


def sigmoid(v):
    return 1.0 / (1.0 + np.exp(-np.maximum(v, -700.0)))


K, T, S, J, H, N = 1024, 1024, 512, 512, 512, 128


def setup_inputs():
    n = np.random.standard_normal
    s = mx_kscale(K)[:, None]
    u = mx_kscale(H)
    r = mx_kscale(J)[:, None]
    return {
        "xT": (n((K, T)) * s).astype(np.float32),
        "eT": (n((J, S)) * r).astype(np.float32),
        "w1": (n((K, H)) / np.sqrt(K) / s * u).astype(np.float32),
        "w3": (n((J, H)) / np.sqrt(J) / r).astype(np.float32),
        "w2": (n((H, N)) / np.sqrt(H) / u[:, None]).astype(np.float32),
        "offs": striped(np.random.permutation(T)[:S]),
    }


def reference(xT, eT, w1, w3, w2, offs):
    c = mxq(f64(w1), 0, "e4m3").T @ mxq(f64(xT)[:, unstriped(offs)], 0, "e4m3")
    z = c * sigmoid(mxq(f64(w3), 0, "e4m3").T @ mxq(f64(eT), 0, "e4m3"))
    return mxq(f64(w2), 0, "e4m3").T @ mxq(z, 0, "e4m3")

@@ -1,0 +1,184 @@
+from contextlib import ExitStack
+
+import concourse.mybir as mybir
+
+F32 = mybir.dt.float32
+BF16 = mybir.dt.bfloat16
+U32 = mybir.dt.uint32
+U16 = mybir.dt.uint16
+U8 = mybir.dt.uint8
+FP8X4 = mybir.dt.float8_e4m3fn_x4
+SIGMOID = mybir.ActivationFunctionType.Sigmoid
+MULT = mybir.AluOpType.mult
+
+K, T, S, J, H, N = 1024, 1024, 512, 512, 512, 128
+FLOPS = 2 * S * (K * H + J * H + H * N)
+
+P = 128
+PACK = 4
+K_PASS = P * PACK
+CHUNK = 128
+
+X_SCALAR = 336
+W_SCALAR = 84
+E_SCALAR = 160
+
+
+def tile_picked_schnet_sigmoid_e_kernel(tc, xT, eT, w1, w3, w2, offs, out):
+    nc = tc.nc
+
+    def rows_of_4(dram):
+        return dram.rearrange("(p j) w -> p j w", j=PACK)
+
+    def cast_columns(raw, grouped, scalar_width, width):
+        dst = grouped[:].rearrange("p (c i) t -> p c t i", i=4)
+        src = raw[:].rearrange("p t (c i) -> p c t i", i=4)
+        cut = scalar_width // 4
+        if cut > 0:
+            nc.scalar.copy(out=dst[:, :cut], in_=src[:, :cut])
+        if cut < width // 4:
+            nc.vector.tensor_copy(out=dst[:, cut:], in_=src[:, cut:])
+
+    def cast_permuted(raw, grouped, cut):
+        dst = grouped[:].rearrange("p t m j -> p m j t")
+        src = raw[:].rearrange("p j (m t) -> p m j t", t=4)
+        nc.scalar.copy(out=dst[:, :cut], in_=src[:, :cut])
+        nc.vector.tensor_copy(out=dst[:, cut:], in_=src[:, cut:])
+
+    with ExitStack() as ctx:
+        keep = ctx.enter_context(tc.tile_pool(name="keep", bufs=1))
+        psum = ctx.enter_context(tc.psum_pool(name="psum", bufs=1))
+        ring = ctx.enter_context(tc.psum_pool(name="ring", bufs=2))
+
+        offsets = keep.tile([P, S // 16], U16, name="offsets")
+        nc.sync.dma_start(offsets[:], offs)
+
+        x_raw = {}
+        for s in range(2):
+            for h in range(2):
+                x_raw[s, h] = keep.tile([P, PACK, 512], F32, name=f"x_raw_{s}_{h}", align_bytes=64)
+                nc.sync.dma_start(
+                    out=x_raw[s, h][:], in_=rows_of_4(xT[s * K_PASS : (s + 1) * K_PASS, h * 512 : (h + 1) * 512])
+                )
+        w1_raw = {}
+        for s in range(2):
+            w1_raw[s] = keep.tile([P, PACK, H], F32, name=f"w1_raw_{s}", align_bytes=64)
+            nc.sync.dma_start(out=w1_raw[s][:], in_=rows_of_4(w1[s * K_PASS : (s + 1) * K_PASS, :]))
+        w2_raw = keep.tile([P, PACK, N], F32, name="w2_raw", align_bytes=64)
+        nc.sync.dma_start(out=w2_raw[:], in_=rows_of_4(w2))
+        w3_raw = keep.tile([P, PACK, H], F32, name="w3_raw", align_bytes=64)
+        nc.sync.dma_start(out=w3_raw[:], in_=rows_of_4(w3))
+        e_raw = {}
+        for h in range(2):
+            e_raw[h] = keep.tile([P, PACK, 256], F32, name=f"e_raw_{h}", align_bytes=64)
+            nc.sync.dma_start(out=e_raw[h][:], in_=rows_of_4(eT[:, h * 256 : (h + 1) * 256]))
+
+        warm = keep.tile([P, 1], F32, name="warm")
+        nc.vector.memset(warm[:], 0.0)
+        nc.scalar.activation(out=warm[:], in_=warm[:], func=SIGMOID)
+
+        x_scales = keep.tile([P, T], U8, name="x_scales", align_bytes=64)
+        nc.gpsimd.memset(x_scales[:], 0)
+        g_scales = keep.tile([P, S], U8, name="g_scales", align_bytes=64)
+        g_codes = {}
+        for s in range(2):
+            x_codes = keep.tile([P, T], U32, name=f"x_codes_{s}", align_bytes=64)
+            for h in range(2):
+                cols = slice(h * 512, (h + 1) * 512)
+                grouped = keep.tile([P, 512, PACK], BF16, name=f"x_grouped_{s}_{h}", align_bytes=64)
+                cast_columns(x_raw[s, h], grouped, X_SCALAR, 512)
+                nc.vector.quantize_mx(
+                    out=x_codes[:, cols].bitcast(FP8X4),
+                    scales=x_scales[4 * s : P, cols],
+                    in_=grouped[:].rearrange("p w t -> p (w t)"),
+                )
+            g_codes[s] = keep.tile([P, S], U32, name=f"g_codes_{s}", align_bytes=64)
+            nc.vector.tensor_copy(out=g_codes[s][:], in_=x_codes[:].indirect(offsets[:]))
+        nc.vector.tensor_copy(out=g_scales[:], in_=x_scales[:].indirect(offsets[:]))
+
+        def weights(raw, name):
+            codes = keep.tile([P, H], U32, name=f"{name}_codes", align_bytes=64)
+            scales = keep.tile([P, H], U8, name=f"{name}_scales", align_bytes=64)
+            grouped = keep.tile([P, PACK, P, PACK], BF16, name=f"{name}_grouped", align_bytes=64)
+            cast_permuted(raw, grouped, W_SCALAR)
+            nc.vector.quantize_mx(
+                out=codes[:].bitcast(FP8X4), scales=scales[:], in_=grouped[:].rearrange("p t m j -> p (t m j)")
+            )
+            return codes, scales
+
+        w1_q = [weights(w1_raw[s], f"w1_{s}") for s in range(2)]
+
+        c_banks = {}
+        for n in range(4):
+            cols = slice(n * CHUNK, (n + 1) * CHUNK)
+            c_banks[n] = psum.tile([P, PACK, CHUNK], F32, name=f"c_{n}")
+            for t in range(PACK):
+                rows = slice(t * P, (t + 1) * P)
+                for s in range(2):
+                    nc.tensor.matmul_mx(
+                        out=c_banks[n][:, t, :],
+                        lhsT=w1_q[s][0][:, rows].bitcast(FP8X4),
+                        lhsT_scale=w1_q[s][1][:, rows],
+                        rhs=g_codes[s][:, cols].bitcast(FP8X4),
+                        rhs_scale=g_scales[4 * s : P, cols],
+                        start=(s == 0),
+                        stop=(s == 1),
+                    )
+
+        w2_codes = keep.tile([P, N], U32, name="w2_codes", align_bytes=64)
+        w2_scales = keep.tile([P, N], U8, name="w2_scales", align_bytes=64)
+        w2_grouped = keep.tile([P, N, PACK], BF16, name="w2_grouped", align_bytes=64)
+        cast_columns(w2_raw, w2_grouped, 0, N)
+        nc.vector.quantize_mx(
+            out=w2_codes[:].bitcast(FP8X4), scales=w2_scales[:], in_=w2_grouped[:].rearrange("p w t -> p (w t)")
+        )
+
+        w3_codes, w3_scales = weights(w3_raw, "w3")
+
+        for h in range(2):
+            e_codes = keep.tile([P, 256], U32, name=f"e_codes_{h}", align_bytes=64)
+            e_scales = keep.tile([P, 256], U8, name=f"e_scales_{h}", align_bytes=64)
+            e_grouped = keep.tile([P, 256, PACK], BF16, name=f"e_grouped_{h}", align_bytes=64)
+            cast_columns(e_raw[h], e_grouped, E_SCALAR, 256)
+            nc.vector.quantize_mx(
+                out=e_codes[:].bitcast(FP8X4), scales=e_scales[:], in_=e_grouped[:].rearrange("p w t -> p (w t)")
+            )
+            for q in range(2):
+                n = 2 * h + q
+                part = slice(q * CHUNK, (q + 1) * CHUNK)
+                f_bank = ring.tile([P, PACK, CHUNK], F32, name="f_bank")
+                for t in range(PACK):
+                    rows = slice(t * P, (t + 1) * P)
+                    nc.tensor.matmul_mx(
+                        out=f_bank[:, t, :],
+                        lhsT=w3_codes[:, rows].bitcast(FP8X4),
+                        lhsT_scale=w3_scales[:, rows],
+                        rhs=e_codes[:, part].bitcast(FP8X4),
+                        rhs_scale=e_scales[:, part],
+                        start=True,
+                        stop=True,
+                    )
+                gate = keep.tile([P, CHUNK, PACK], F32, name=f"gate_{n}", align_bytes=64)
+                nc.scalar.activation(out=gate[:], in_=f_bank[:].rearrange("p t n -> p n t"), func=SIGMOID)
+                z = keep.tile([P, CHUNK, PACK], BF16, name=f"z_{n}", align_bytes=64)
+                nc.vector.tensor_tensor(
+                    out=z[:], in0=c_banks[n][:].rearrange("p t n -> p n t"), in1=gate[:], op=MULT
+                )
+                z_codes = keep.tile([P, CHUNK], U32, name=f"z_codes_{n}", align_bytes=64)
+                z_scales = keep.tile([P, CHUNK], U8, name=f"z_scales_{n}", align_bytes=64)
+                nc.vector.quantize_mx(
+                    out=z_codes[:].bitcast(FP8X4), scales=z_scales[:], in_=z[:].rearrange("p n t -> p (n t)")
+                )
+                o_bank = ring.tile([P, CHUNK], F32, name="o_bank")
+                nc.tensor.matmul_mx(
+                    out=o_bank[:],
+                    lhsT=w2_codes[:].bitcast(FP8X4),
+                    lhsT_scale=w2_scales[:],
+                    rhs=z_codes[:].bitcast(FP8X4),
+                    rhs_scale=z_scales[:],
+                    start=True,
+                    stop=True,
+                )
+                result = keep.tile([P, CHUNK], F32, name=f"result_{n}")
+                nc.scalar.copy(out=result[:], in_=o_bank[:])
+                nc.sync.dma_start(out=out[:, n * CHUNK : (n + 1) * CHUNK], in_=result[:])

@@ -19,9 +19,11 @@ PACK = 4
 K_PASS = P * PACK
 CHUNK = 128
 
-X_SCALAR = 336
-W_SCALAR = 84
-E_SCALAR = 160
+X_SCALAR = (176, 176, 176, 176)
+W1_SCALAR = (116, 96)
+W3_SCALAR = 72
+E_SCALAR = (96, 96)
+W2_SCALAR = 0
 
 
 def tile_picked_schnet_sigmoid_e_kernel(tc, xT, eT, w1, w3, w2, offs, out):
@@ -30,20 +32,19 @@ def tile_picked_schnet_sigmoid_e_kernel(tc, xT, eT, w1, w3, w2, offs, out):
     def rows_of_4(dram):
         return dram.rearrange("(p j) w -> p j w", j=PACK)
 
-    def cast_columns(raw, grouped, scalar_width, width):
-        dst = grouped[:].rearrange("p (c i) t -> p c t i", i=4)
-        src = raw[:].rearrange("p t (c i) -> p c t i", i=4)
+    def cast_columns(dst, src, width, scalar_width):
+        dst = dst.rearrange("p (c i) t -> p c t i", i=4)
+        src = src.rearrange("p t (c i) -> p c t i", i=4)
         cut = scalar_width // 4
         if cut > 0:
             nc.scalar.copy(out=dst[:, :cut], in_=src[:, :cut])
         if cut < width // 4:
             nc.vector.tensor_copy(out=dst[:, cut:], in_=src[:, cut:])
 
-    def cast_permuted(raw, grouped, cut):
-        dst = grouped[:].rearrange("p t m j -> p m j t")
-        src = raw[:].rearrange("p j (m t) -> p m j t", t=4)
-        nc.scalar.copy(out=dst[:, :cut], in_=src[:, :cut])
-        nc.vector.tensor_copy(out=dst[:, cut:], in_=src[:, cut:])
+    def load(dram, shape, name):
+        raw = keep.tile(shape, F32, name=name, align_bytes=64)
+        nc.sync.dma_start(out=raw[:], in_=rows_of_4(dram))
+        return raw
 
     with ExitStack() as ctx:
         keep = ctx.enter_context(tc.tile_pool(name="keep", bufs=1))
@@ -51,27 +52,13 @@ def tile_picked_schnet_sigmoid_e_kernel(tc, xT, eT, w1, w3, w2, offs, out):
         ring = ctx.enter_context(tc.psum_pool(name="ring", bufs=2))
 
         offsets = keep.tile([P, S // 16], U16, name="offsets")
+        x_raw = [load(xT[:K_PASS, :], [P, PACK, T], "x_raw_0")]
         nc.sync.dma_start(offsets[:], offs)
-
-        x_raw = {}
-        for s in range(2):
-            for h in range(2):
-                x_raw[s, h] = keep.tile([P, PACK, 512], F32, name=f"x_raw_{s}_{h}", align_bytes=64)
-                nc.sync.dma_start(
-                    out=x_raw[s, h][:], in_=rows_of_4(xT[s * K_PASS : (s + 1) * K_PASS, h * 512 : (h + 1) * 512])
-                )
-        w1_raw = {}
-        for s in range(2):
-            w1_raw[s] = keep.tile([P, PACK, H], F32, name=f"w1_raw_{s}", align_bytes=64)
-            nc.sync.dma_start(out=w1_raw[s][:], in_=rows_of_4(w1[s * K_PASS : (s + 1) * K_PASS, :]))
-        w2_raw = keep.tile([P, PACK, N], F32, name="w2_raw", align_bytes=64)
-        nc.sync.dma_start(out=w2_raw[:], in_=rows_of_4(w2))
-        w3_raw = keep.tile([P, PACK, H], F32, name="w3_raw", align_bytes=64)
-        nc.sync.dma_start(out=w3_raw[:], in_=rows_of_4(w3))
-        e_raw = {}
-        for h in range(2):
-            e_raw[h] = keep.tile([P, PACK, 256], F32, name=f"e_raw_{h}", align_bytes=64)
-            nc.sync.dma_start(out=e_raw[h][:], in_=rows_of_4(eT[:, h * 256 : (h + 1) * 256]))
+        x_raw.append(load(xT[K_PASS:, :], [P, PACK, T], "x_raw_1"))
+        w1_raw = [load(w1[s * K_PASS : (s + 1) * K_PASS, :], [P, PACK, H], f"w1_raw_{s}") for s in range(2)]
+        w3_raw = load(w3, [P, PACK, H], "w3_raw")
+        e_raw = [load(eT[:, h * 256 : (h + 1) * 256], [P, PACK, 256], f"e_raw_{h}") for h in range(2)]
+        w2_raw = load(w2, [P, PACK, N], "w2_raw")
 
         warm = keep.tile([P, 1], F32, name="warm")
         nc.vector.memset(warm[:], 0.0)
@@ -80,36 +67,51 @@ def tile_picked_schnet_sigmoid_e_kernel(tc, xT, eT, w1, w3, w2, offs, out):
         x_scales = keep.tile([P, T], U8, name="x_scales", align_bytes=64)
         nc.gpsimd.memset(x_scales[:], 0)
         g_scales = keep.tile([P, S], U8, name="g_scales", align_bytes=64)
-        g_codes = {}
-        for s in range(2):
-            x_codes = keep.tile([P, T], U32, name=f"x_codes_{s}", align_bytes=64)
+        x_codes = [keep.tile([P, T], U32, name=f"x_codes_{s}", align_bytes=64) for s in range(2)]
+        g_codes = [keep.tile([P, S], U32, name=f"g_codes_{s}", align_bytes=64) for s in range(2)]
+
+        def quantize_atoms(s):
+            grouped = keep.tile([P, T, PACK], BF16, name=f"x_grouped_{s}", align_bytes=64)
             for h in range(2):
                 cols = slice(h * 512, (h + 1) * 512)
-                grouped = keep.tile([P, 512, PACK], BF16, name=f"x_grouped_{s}_{h}", align_bytes=64)
-                cast_columns(x_raw[s, h], grouped, X_SCALAR, 512)
+                cast_columns(grouped[:, cols, :], x_raw[s][:, :, cols], 512, X_SCALAR[2 * s + h])
+            for h in range(2):
+                cols = slice(h * 512, (h + 1) * 512)
                 nc.vector.quantize_mx(
-                    out=x_codes[:, cols].bitcast(FP8X4),
+                    out=x_codes[s][:, cols].bitcast(FP8X4),
                     scales=x_scales[4 * s : P, cols],
-                    in_=grouped[:].rearrange("p w t -> p (w t)"),
+                    in_=grouped[:, cols, :].rearrange("p w t -> p (w t)"),
                 )
-            g_codes[s] = keep.tile([P, S], U32, name=f"g_codes_{s}", align_bytes=64)
-            nc.vector.tensor_copy(out=g_codes[s][:], in_=x_codes[:].indirect(offsets[:]))
-        nc.vector.tensor_copy(out=g_scales[:], in_=x_scales[:].indirect(offsets[:]))
 
-        def weights(raw, name):
+        def gather_codes(s):
+            nc.vector.tensor_copy(out=g_codes[s][:], in_=x_codes[s][:].indirect(offsets[:]))
+
+        quantize_atoms(0)
+        gather_codes(0)
+        quantize_atoms(1)
+
+        def weights(raw, name, cut):
             codes = keep.tile([P, H], U32, name=f"{name}_codes", align_bytes=64)
             scales = keep.tile([P, H], U8, name=f"{name}_scales", align_bytes=64)
             grouped = keep.tile([P, PACK, P, PACK], BF16, name=f"{name}_grouped", align_bytes=64)
-            cast_permuted(raw, grouped, W_SCALAR)
+            dst = grouped[:].rearrange("p t m j -> p m j t")
+            src = raw[:].rearrange("p j (m t) -> p m j t", t=PACK)
+            nc.scalar.copy(out=dst[:, :cut], in_=src[:, :cut])
+            nc.vector.tensor_copy(out=dst[:, cut:], in_=src[:, cut:])
             nc.vector.quantize_mx(
                 out=codes[:].bitcast(FP8X4), scales=scales[:], in_=grouped[:].rearrange("p t m j -> p (t m j)")
             )
             return codes, scales
 
-        w1_q = [weights(w1_raw[s], f"w1_{s}") for s in range(2)]
+        w1_q = [weights(w1_raw[0], "w1_0", W1_SCALAR[0])]
+        nc.vector.tensor_copy(out=g_scales[:], in_=x_scales[:].indirect(offsets[:]))
+        gather_codes(1)
+        w1_q.append(weights(w1_raw[1], "w1_1", W1_SCALAR[1]))
+        w3_codes, w3_scales = weights(w3_raw, "w3", W3_SCALAR)
 
         c_banks = {}
-        for n in range(4):
+
+        def product_c(n):
             cols = slice(n * CHUNK, (n + 1) * CHUNK)
             c_banks[n] = psum.tile([P, PACK, CHUNK], F32, name=f"c_{n}")
             for t in range(PACK):
@@ -125,60 +127,90 @@ def tile_picked_schnet_sigmoid_e_kernel(tc, xT, eT, w1, w3, w2, offs, out):
                         stop=(s == 1),
                     )
 
-        w2_codes = keep.tile([P, N], U32, name="w2_codes", align_bytes=64)
-        w2_scales = keep.tile([P, N], U8, name="w2_scales", align_bytes=64)
-        w2_grouped = keep.tile([P, N, PACK], BF16, name="w2_grouped", align_bytes=64)
-        cast_columns(w2_raw, w2_grouped, 0, N)
-        nc.vector.quantize_mx(
-            out=w2_codes[:].bitcast(FP8X4), scales=w2_scales[:], in_=w2_grouped[:].rearrange("p w t -> p (w t)")
-        )
+        e_codes = [keep.tile([P, 256], U32, name=f"e_codes_{h}", align_bytes=64) for h in range(2)]
+        e_scales = [keep.tile([P, 256], U8, name=f"e_scales_{h}", align_bytes=64) for h in range(2)]
 
-        w3_codes, w3_scales = weights(w3_raw, "w3")
-
-        for h in range(2):
-            e_codes = keep.tile([P, 256], U32, name=f"e_codes_{h}", align_bytes=64)
-            e_scales = keep.tile([P, 256], U8, name=f"e_scales_{h}", align_bytes=64)
-            e_grouped = keep.tile([P, 256, PACK], BF16, name=f"e_grouped_{h}", align_bytes=64)
-            cast_columns(e_raw[h], e_grouped, E_SCALAR, 256)
-            nc.vector.quantize_mx(
-                out=e_codes[:].bitcast(FP8X4), scales=e_scales[:], in_=e_grouped[:].rearrange("p w t -> p (w t)")
-            )
+        def edges(h):
+            grouped = keep.tile([P, 256, PACK], BF16, name=f"e_grouped_{h}", align_bytes=64)
+            cast_columns(grouped[:], e_raw[h][:], 256, E_SCALAR[h])
             for q in range(2):
-                n = 2 * h + q
                 part = slice(q * CHUNK, (q + 1) * CHUNK)
-                f_bank = ring.tile([P, PACK, CHUNK], F32, name="f_bank")
-                for t in range(PACK):
-                    rows = slice(t * P, (t + 1) * P)
-                    nc.tensor.matmul_mx(
-                        out=f_bank[:, t, :],
-                        lhsT=w3_codes[:, rows].bitcast(FP8X4),
-                        lhsT_scale=w3_scales[:, rows],
-                        rhs=e_codes[:, part].bitcast(FP8X4),
-                        rhs_scale=e_scales[:, part],
-                        start=True,
-                        stop=True,
-                    )
-                gate = keep.tile([P, CHUNK, PACK], F32, name=f"gate_{n}", align_bytes=64)
-                nc.scalar.activation(out=gate[:], in_=f_bank[:].rearrange("p t n -> p n t"), func=SIGMOID)
-                z = keep.tile([P, CHUNK, PACK], BF16, name=f"z_{n}", align_bytes=64)
-                nc.vector.tensor_tensor(
-                    out=z[:], in0=c_banks[n][:].rearrange("p t n -> p n t"), in1=gate[:], op=MULT
-                )
-                z_codes = keep.tile([P, CHUNK], U32, name=f"z_codes_{n}", align_bytes=64)
-                z_scales = keep.tile([P, CHUNK], U8, name=f"z_scales_{n}", align_bytes=64)
                 nc.vector.quantize_mx(
-                    out=z_codes[:].bitcast(FP8X4), scales=z_scales[:], in_=z[:].rearrange("p n t -> p (n t)")
+                    out=e_codes[h][:, part].bitcast(FP8X4),
+                    scales=e_scales[h][:, part],
+                    in_=grouped[:, part, :].rearrange("p w t -> p (w t)"),
                 )
-                o_bank = ring.tile([P, CHUNK], F32, name="o_bank")
+
+        gates = {}
+
+        def gate(n):
+            h, q = divmod(n, 2)
+            part = slice(q * CHUNK, (q + 1) * CHUNK)
+            f_bank = ring.tile([P, PACK, CHUNK], F32, name="f_bank")
+            for t in range(PACK):
+                rows = slice(t * P, (t + 1) * P)
                 nc.tensor.matmul_mx(
-                    out=o_bank[:],
-                    lhsT=w2_codes[:].bitcast(FP8X4),
-                    lhsT_scale=w2_scales[:],
-                    rhs=z_codes[:].bitcast(FP8X4),
-                    rhs_scale=z_scales[:],
+                    out=f_bank[:, t, :],
+                    lhsT=w3_codes[:, rows].bitcast(FP8X4),
+                    lhsT_scale=w3_scales[:, rows],
+                    rhs=e_codes[h][:, part].bitcast(FP8X4),
+                    rhs_scale=e_scales[h][:, part],
                     start=True,
                     stop=True,
                 )
-                result = keep.tile([P, CHUNK], F32, name=f"result_{n}")
-                nc.scalar.copy(out=result[:], in_=o_bank[:])
-                nc.sync.dma_start(out=out[:, n * CHUNK : (n + 1) * CHUNK], in_=result[:])
+            gates[n] = keep.tile([P, CHUNK, PACK], F32, name=f"gate_{n}", align_bytes=64)
+            nc.scalar.activation(out=gates[n][:], in_=f_bank[:].rearrange("p t n -> p n t"), func=SIGMOID)
+
+        z_codes = {}
+        z_scales = {}
+
+        def message(n):
+            z = keep.tile([P, CHUNK, PACK], BF16, name=f"z_{n}", align_bytes=64)
+            nc.vector.tensor_tensor(
+                out=z[:], in0=c_banks[n][:].rearrange("p t n -> p n t"), in1=gates[n][:], op=MULT
+            )
+            z_codes[n] = keep.tile([P, CHUNK], U32, name=f"z_codes_{n}", align_bytes=64)
+            z_scales[n] = keep.tile([P, CHUNK], U8, name=f"z_scales_{n}", align_bytes=64)
+            nc.vector.quantize_mx(
+                out=z_codes[n][:].bitcast(FP8X4), scales=z_scales[n][:], in_=z[:].rearrange("p n t -> p (n t)")
+            )
+
+        w2_codes = keep.tile([P, N], U32, name="w2_codes", align_bytes=64)
+        w2_scales = keep.tile([P, N], U8, name="w2_scales", align_bytes=64)
+
+        def project(n):
+            o_bank = ring.tile([P, CHUNK], F32, name="o_bank")
+            nc.tensor.matmul_mx(
+                out=o_bank[:],
+                lhsT=w2_codes[:].bitcast(FP8X4),
+                lhsT_scale=w2_scales[:],
+                rhs=z_codes[n][:].bitcast(FP8X4),
+                rhs_scale=z_scales[n][:],
+                start=True,
+                stop=True,
+            )
+            result = keep.tile([P, CHUNK], F32, name=f"result_{n}")
+            nc.scalar.copy(out=result[:], in_=o_bank[:])
+            nc.sync.dma_start(out=out[:, n * CHUNK : (n + 1) * CHUNK], in_=result[:])
+
+        edges(0)
+        product_c(0)
+        gate(0)
+        gate(1)
+        edges(1)
+        product_c(1)
+        message(0)
+        w2_grouped = keep.tile([P, N, PACK], BF16, name="w2_grouped", align_bytes=64)
+        cast_columns(w2_grouped[:], w2_raw[:], N, W2_SCALAR)
+        nc.vector.quantize_mx(
+            out=w2_codes[:].bitcast(FP8X4), scales=w2_scales[:], in_=w2_grouped[:].rearrange("p w t -> p (w t)")
+        )
+        gate(2)
+        product_c(2)
+        message(1)
+        gate(3)
+        product_c(3)
+        message(2)
+        message(3)
+        for n in range(4):
+            project(n)

@@ -18,11 +18,12 @@ P = 128
 PACK = 4
 K_PASS = P * PACK
 CHUNK = 128
+HALVES = (slice(0, 128),)
 
-X_SCALAR = (176, 176, 176, 176)
-W1_SCALAR = (116, 96)
-W3_SCALAR = 72
-E_SCALAR = (96, 96)
+X_SCALAR = (264, 264, 264, 264)
+W1_SCALAR = (92, 116)
+W3_SCALAR = 104
+E_SCALAR = (96, 160)
 W2_SCALAR = 0
 
 
@@ -159,16 +160,23 @@ def tile_picked_schnet_sigmoid_e_kernel(tc, xT, eT, w1, w3, w2, offs, out):
                     stop=True,
                 )
             gates[n] = keep.tile([P, CHUNK, PACK], F32, name=f"gate_{n}", align_bytes=64)
-            nc.scalar.activation(out=gates[n][:], in_=f_bank[:].rearrange("p t n -> p n t"), func=SIGMOID)
+            for half in HALVES:
+                nc.scalar.activation(
+                    out=gates[n][:, half, :], in_=f_bank[:, :, half].rearrange("p t n -> p n t"), func=SIGMOID
+                )
 
         z_codes = {}
         z_scales = {}
 
         def message(n):
             z = keep.tile([P, CHUNK, PACK], BF16, name=f"z_{n}", align_bytes=64)
-            nc.vector.tensor_tensor(
-                out=z[:], in0=c_banks[n][:].rearrange("p t n -> p n t"), in1=gates[n][:], op=MULT
-            )
+            for half in HALVES:
+                nc.vector.tensor_tensor(
+                    out=z[:, half, :],
+                    in0=c_banks[n][:, :, half].rearrange("p t n -> p n t"),
+                    in1=gates[n][:, half, :],
+                    op=MULT,
+                )
             z_codes[n] = keep.tile([P, CHUNK], U32, name=f"z_codes_{n}", align_bytes=64)
             z_scales[n] = keep.tile([P, CHUNK], U8, name=f"z_scales_{n}", align_bytes=64)
             nc.vector.quantize_mx(
@@ -195,10 +203,10 @@ def tile_picked_schnet_sigmoid_e_kernel(tc, xT, eT, w1, w3, w2, offs, out):
 
         edges(0)
         product_c(0)
+        product_c(1)
         gate(0)
         gate(1)
         edges(1)
-        product_c(1)
         message(0)
         w2_grouped = keep.tile([P, N, PACK], BF16, name="w2_grouped", align_bytes=64)
         cast_columns(w2_grouped[:], w2_raw[:], N, W2_SCALAR)

from contextlib import ExitStack

import concourse.mybir as mybir

F32 = mybir.dt.float32
BF16 = mybir.dt.bfloat16
U32 = mybir.dt.uint32
U16 = mybir.dt.uint16
U8 = mybir.dt.uint8
FP8X4 = mybir.dt.float8_e4m3fn_x4
SIGMOID = mybir.ActivationFunctionType.Sigmoid
MULT = mybir.AluOpType.mult

K, T, S, J, H, N = 1024, 1024, 512, 512, 512, 128
FLOPS = 2 * S * (K * H + J * H + H * N)

P = 128
PACK = 4
K_PASS = P * PACK
CHUNK = 128
HALVES = (slice(0, 128),)

X_SCALAR = (264, 264, 264, 264)
W1_SCALAR = (92, 116)
W3_SCALAR = 104
E_SCALAR = (96, 160)
W2_SCALAR = 0


def tile_picked_schnet_sigmoid_e_kernel(tc, xT, eT, w1, w3, w2, offs, out):
    nc = tc.nc

    def rows_of_4(dram):
        return dram.rearrange("(p j) w -> p j w", j=PACK)

    def cast_columns(dst, src, width, scalar_width):
        dst = dst.rearrange("p (c i) t -> p c t i", i=4)
        src = src.rearrange("p t (c i) -> p c t i", i=4)
        cut = scalar_width // 4
        if cut > 0:
            nc.scalar.copy(out=dst[:, :cut], in_=src[:, :cut])
        if cut < width // 4:
            nc.vector.tensor_copy(out=dst[:, cut:], in_=src[:, cut:])

    def load(dram, shape, name):
        raw = keep.tile(shape, F32, name=name, align_bytes=64)
        nc.sync.dma_start(out=raw[:], in_=rows_of_4(dram))
        return raw

    with ExitStack() as ctx:
        keep = ctx.enter_context(tc.tile_pool(name="keep", bufs=1))
        psum = ctx.enter_context(tc.psum_pool(name="psum", bufs=1))
        ring = ctx.enter_context(tc.psum_pool(name="ring", bufs=2))

        offsets = keep.tile([P, S // 16], U16, name="offsets")
        x_raw = [load(xT[:K_PASS, :], [P, PACK, T], "x_raw_0")]
        nc.sync.dma_start(offsets[:], offs)
        x_raw.append(load(xT[K_PASS:, :], [P, PACK, T], "x_raw_1"))
        w1_raw = [load(w1[s * K_PASS : (s + 1) * K_PASS, :], [P, PACK, H], f"w1_raw_{s}") for s in range(2)]
        w3_raw = load(w3, [P, PACK, H], "w3_raw")
        e_raw = [load(eT[:, h * 256 : (h + 1) * 256], [P, PACK, 256], f"e_raw_{h}") for h in range(2)]
        w2_raw = load(w2, [P, PACK, N], "w2_raw")

        warm = keep.tile([P, 1], F32, name="warm")
        nc.vector.memset(warm[:], 0.0)
        nc.scalar.activation(out=warm[:], in_=warm[:], func=SIGMOID)

        x_scales = keep.tile([P, T], U8, name="x_scales", align_bytes=64)
        nc.gpsimd.memset(x_scales[:], 0)
        g_scales = keep.tile([P, S], U8, name="g_scales", align_bytes=64)
        x_codes = [keep.tile([P, T], U32, name=f"x_codes_{s}", align_bytes=64) for s in range(2)]
        g_codes = [keep.tile([P, S], U32, name=f"g_codes_{s}", align_bytes=64) for s in range(2)]

        def quantize_atoms(s):
            grouped = keep.tile([P, T, PACK], BF16, name=f"x_grouped_{s}", align_bytes=64)
            for h in range(2):
                cols = slice(h * 512, (h + 1) * 512)
                cast_columns(grouped[:, cols, :], x_raw[s][:, :, cols], 512, X_SCALAR[2 * s + h])
            for h in range(2):
                cols = slice(h * 512, (h + 1) * 512)
                nc.vector.quantize_mx(
                    out=x_codes[s][:, cols].bitcast(FP8X4),
                    scales=x_scales[4 * s : P, cols],
                    in_=grouped[:, cols, :].rearrange("p w t -> p (w t)"),
                )

        def gather_codes(s):
            nc.vector.tensor_copy(out=g_codes[s][:], in_=x_codes[s][:].indirect(offsets[:]))

        quantize_atoms(0)
        gather_codes(0)
        quantize_atoms(1)

        def weights(raw, name, cut):
            codes = keep.tile([P, H], U32, name=f"{name}_codes", align_bytes=64)
            scales = keep.tile([P, H], U8, name=f"{name}_scales", align_bytes=64)
            grouped = keep.tile([P, PACK, P, PACK], BF16, name=f"{name}_grouped", align_bytes=64)
            dst = grouped[:].rearrange("p t m j -> p m j t")
            src = raw[:].rearrange("p j (m t) -> p m j t", t=PACK)
            nc.scalar.copy(out=dst[:, :cut], in_=src[:, :cut])
            nc.vector.tensor_copy(out=dst[:, cut:], in_=src[:, cut:])
            nc.vector.quantize_mx(
                out=codes[:].bitcast(FP8X4), scales=scales[:], in_=grouped[:].rearrange("p t m j -> p (t m j)")
            )
            return codes, scales

        w1_q = [weights(w1_raw[0], "w1_0", W1_SCALAR[0])]
        nc.vector.tensor_copy(out=g_scales[:], in_=x_scales[:].indirect(offsets[:]))
        gather_codes(1)
        w1_q.append(weights(w1_raw[1], "w1_1", W1_SCALAR[1]))
        w3_codes, w3_scales = weights(w3_raw, "w3", W3_SCALAR)

        c_banks = {}

        def product_c(n):
            cols = slice(n * CHUNK, (n + 1) * CHUNK)
            c_banks[n] = psum.tile([P, PACK, CHUNK], F32, name=f"c_{n}")
            for t in range(PACK):
                rows = slice(t * P, (t + 1) * P)
                for s in range(2):
                    nc.tensor.matmul_mx(
                        out=c_banks[n][:, t, :],
                        lhsT=w1_q[s][0][:, rows].bitcast(FP8X4),
                        lhsT_scale=w1_q[s][1][:, rows],
                        rhs=g_codes[s][:, cols].bitcast(FP8X4),
                        rhs_scale=g_scales[4 * s : P, cols],
                        start=(s == 0),
                        stop=(s == 1),
                    )

        e_codes = [keep.tile([P, 256], U32, name=f"e_codes_{h}", align_bytes=64) for h in range(2)]
        e_scales = [keep.tile([P, 256], U8, name=f"e_scales_{h}", align_bytes=64) for h in range(2)]

        def edges(h):
            grouped = keep.tile([P, 256, PACK], BF16, name=f"e_grouped_{h}", align_bytes=64)
            cast_columns(grouped[:], e_raw[h][:], 256, E_SCALAR[h])
            for q in range(2):
                part = slice(q * CHUNK, (q + 1) * CHUNK)
                nc.vector.quantize_mx(
                    out=e_codes[h][:, part].bitcast(FP8X4),
                    scales=e_scales[h][:, part],
                    in_=grouped[:, part, :].rearrange("p w t -> p (w t)"),
                )

        gates = {}

        def gate(n):
            h, q = divmod(n, 2)
            part = slice(q * CHUNK, (q + 1) * CHUNK)
            f_bank = ring.tile([P, PACK, CHUNK], F32, name="f_bank")
            for t in range(PACK):
                rows = slice(t * P, (t + 1) * P)
                nc.tensor.matmul_mx(
                    out=f_bank[:, t, :],
                    lhsT=w3_codes[:, rows].bitcast(FP8X4),
                    lhsT_scale=w3_scales[:, rows],
                    rhs=e_codes[h][:, part].bitcast(FP8X4),
                    rhs_scale=e_scales[h][:, part],
                    start=True,
                    stop=True,
                )
            gates[n] = keep.tile([P, CHUNK, PACK], F32, name=f"gate_{n}", align_bytes=64)
            for half in HALVES:
                nc.scalar.activation(
                    out=gates[n][:, half, :], in_=f_bank[:, :, half].rearrange("p t n -> p n t"), func=SIGMOID
                )

        z_codes = {}
        z_scales = {}

        def message(n):
            z = keep.tile([P, CHUNK, PACK], BF16, name=f"z_{n}", align_bytes=64)
            for half in HALVES:
                nc.vector.tensor_tensor(
                    out=z[:, half, :],
                    in0=c_banks[n][:, :, half].rearrange("p t n -> p n t"),
                    in1=gates[n][:, half, :],
                    op=MULT,
                )
            z_codes[n] = keep.tile([P, CHUNK], U32, name=f"z_codes_{n}", align_bytes=64)
            z_scales[n] = keep.tile([P, CHUNK], U8, name=f"z_scales_{n}", align_bytes=64)
            nc.vector.quantize_mx(
                out=z_codes[n][:].bitcast(FP8X4), scales=z_scales[n][:], in_=z[:].rearrange("p n t -> p (n t)")
            )

        w2_codes = keep.tile([P, N], U32, name="w2_codes", align_bytes=64)
        w2_scales = keep.tile([P, N], U8, name="w2_scales", align_bytes=64)

        def project(n):
            o_bank = ring.tile([P, CHUNK], F32, name="o_bank")
            nc.tensor.matmul_mx(
                out=o_bank[:],
                lhsT=w2_codes[:].bitcast(FP8X4),
                lhsT_scale=w2_scales[:],
                rhs=z_codes[n][:].bitcast(FP8X4),
                rhs_scale=z_scales[n][:],
                start=True,
                stop=True,
            )
            result = keep.tile([P, CHUNK], F32, name=f"result_{n}")
            nc.scalar.copy(out=result[:], in_=o_bank[:])
            nc.sync.dma_start(out=out[:, n * CHUNK : (n + 1) * CHUNK], in_=result[:])

        edges(0)
        product_c(0)
        product_c(1)
        gate(0)
        gate(1)
        edges(1)
        message(0)
        w2_grouped = keep.tile([P, N, PACK], BF16, name="w2_grouped", align_bytes=64)
        cast_columns(w2_grouped[:], w2_raw[:], N, W2_SCALAR)
        nc.vector.quantize_mx(
            out=w2_codes[:].bitcast(FP8X4), scales=w2_scales[:], in_=w2_grouped[:].rearrange("p w t -> p (w t)")
        )
        gate(2)
        product_c(2)
        message(1)
        gate(3)
        product_c(3)
        message(2)
        message(3)
        for n in range(4):
            project(n)
